import numpy as np
import ml_dtypes


def mxq(x, axis, fmt="e4m3"):
    dtype, down = {"e4m3": (ml_dtypes.float8_e4m3fn, 7), "e5m2": (ml_dtypes.float8_e5m2, 14)}[fmt]
    v = np.moveaxis(np.asarray(x, np.float32).astype(ml_dtypes.bfloat16).astype(np.float64), axis, -1)
    blocks = v.reshape(v.shape[:-1] + (-1, 32))
    amax = np.abs(blocks).max(-1, keepdims=True)
    byte = np.maximum(np.where(amax > 0, np.frexp(amax)[1] - 1 + 127, 0) - down, 1)
    scale = np.exp2(byte - 127.0)
    codes = (blocks / scale).astype(np.float32).astype(dtype).astype(np.float64)
    return np.moveaxis((codes * scale).reshape(v.shape), -1, axis)


WIDE = False


def mx_kscale(k):
    if not WIDE:
        return np.ones(k)
    levels = np.array([10, -10, 5, -5, 0])
    if k % 512:
        return np.exp2(np.random.permutation(np.resize(levels, k // 32))).repeat(32)
    a = np.empty((k // 512, 16))
    for p in range(k // 512):
        a[p, :8] = np.random.permutation(np.resize(levels, 8))
        for g in range(8):
            far = levels[np.abs(levels - a[p, g]) >= 10]
            a[p, g + 8] = far[np.random.randint(len(far))]
    return np.exp2(a.ravel()).repeat(32)


def f64(x):
    return np.asarray(x).astype(np.float64)


def striped(idx):
    return np.tile(idx.reshape(-1, 16).T, (8, 1)).astype(np.uint16)


def unstriped(offs):
    return offs[:16].T.reshape(-1).astype(np.int64)


E2M1 = np.array([0.0, 0.5, 1.0, 1.5, 2.0, 3.0, 4.0, 6.0, -0.0, -0.5, -1.0, -1.5, -2.0, -3.0, -4.0, -6.0])


def pack_weight(w, fmt):
    k, n = w.shape
    w = f64(np.asarray(w, np.float32).astype(ml_dtypes.bfloat16)).reshape(k // 32, 32, n)
    amax = np.abs(w).max(1)
    if fmt == "e4m3":
        byte = np.frexp(amax)[1] - 1 + 127 - 7
    else:
        mant, ex = np.frexp(amax / 6.0)
        byte = np.where(mant > 0.5, ex, ex - 1) + 127
    byte = np.clip(np.where(amax > 0, byte, 1), 1, 254)
    scaled = (w * np.exp2(127.0 - byte)[:, None, :]).reshape(k, n).astype(np.float32)
    by_word = np.ascontiguousarray(scaled.reshape(k // 512, 128, 4, n).transpose(0, 1, 3, 2))
    if fmt == "e4m3":
        words = by_word.astype(ml_dtypes.float8_e4m3fn).view(np.uint8)
    else:
        c = by_word.astype(ml_dtypes.float4_e2m1fn).view(np.uint8) & 0xF
        words = (c[..., 0::2] | (c[..., 1::2] << 4)).reshape(k // 512, 128, 2 * n)
    return np.ascontiguousarray(words), np.ascontiguousarray(byte.astype(np.uint8).reshape(k // 512, 16, n))


def unpack_weight(words, scales, fmt):
    g, _, n = scales.shape
    words = np.ascontiguousarray(words).reshape(g, 128, n, -1)
    if fmt == "e4m3":
        vals = words.view(ml_dtypes.float8_e4m3fn).astype(np.float64)
    else:
        nib = np.empty((g, 128, n, 4), np.uint8)
        nib[..., 0::2] = words & 0xF
        nib[..., 1::2] = words >> 4
        vals = E2M1[nib]
    vals = vals * np.repeat(np.exp2(scales.astype(np.float64) - 127.0), 8, axis=1)[..., None]
    return vals.transpose(0, 1, 3, 2).reshape(g * 512, n)


def gelu(v):
    return 0.5 * v * (1.0 + np.tanh(np.sqrt(2.0 / np.pi) * (v + 0.044715 * v**3)))


K, T, S, H, T2, P = 512, 4096, 1024, 1024, 2048, 1024


def setup_inputs():
    n = np.random.standard_normal
    s = mx_kscale(K)[:, None]
    u = mx_kscale(H)[:, None]
    tab_words, tab_scales = pack_weight(n((K, T)) * s, "e4m3")
    whi_words, whi_scales = pack_weight(n((K, H)) / np.sqrt(K) / s * u.T, "e2m1")
    return {
        "tab_words": tab_words, "tab_scales": tab_scales,
        "offs": striped(np.random.permutation(T)[:S]),
        "offs2": striped(np.random.permutation(T2)[:S]),
        "offs3": striped(np.random.permutation(T2)[:P]),
        "wlo": (n((K, H)) / np.sqrt(K) / s * u.T).astype(np.float32),
        "whi_words": whi_words, "whi_scales": whi_scales,
        "bhi": ((0.6 + 0.5 * n(H)) * u[:, 0]).astype(np.float32),
        "page0": (n((H, T2)) * u).astype(np.float32),
        "wread": (n((H, H)) / np.sqrt(H) / u).astype(np.float32),
        "d": (n(H) / u[:, 0]).astype(np.float32),
    }


def reference(tab_words, tab_scales, offs, offs2, offs3, wlo, whi_words, whi_scales, bhi, page0, wread, d):
    v = unpack_weight(tab_words, tab_scales, "e4m3")[:, unstriped(offs)]
    whi = unpack_weight(whi_words, whi_scales, "e2m1")
    lo = mxq(f64(wlo), 0, "e4m3").T @ v
    hi = (whi.T @ v) + f64(bhi)[:, None]
    page = f64(page0).copy()
    l2 = unstriped(offs2)
    page[:, l2] = np.minimum(np.maximum(page[:, l2], lo), hi)
    x = page[:, unstriped(offs3)]
    y = mxq(f64(wread), 0, "e4m3").T @ mxq(x, 0, "e4m3")
    return y + f64(d)[:, None] * x

@@ -1,0 +1,214 @@
+from contextlib import ExitStack
+
+import concourse.mybir as mybir
+
+K, T, S, H, T2, J = 512, 4096, 1024, 1024, 2048, 1024
+FLOPS = 2 * K * H * S * 2 + 2 * H * H * J
+
+F32 = mybir.dt.float32
+BF16 = mybir.dt.bfloat16
+I32 = mybir.dt.int32
+U32 = mybir.dt.uint32
+U16 = mybir.dt.uint16
+U8 = mybir.dt.uint8
+FP8X4 = mybir.dt.float8_e4m3fn_x4
+FP4X4 = mybir.dt.float4_e2m1fn_x4
+ALU = mybir.AluOpType
+COPY = mybir.ActivationFunctionType.Copy
+
+P = 128
+PACK = 4
+PASS = P * PACK
+BANK = 512
+SLICES = H // P
+CHUNK = 256
+ALIGN = 64
+
+
+def tile_list_lifeboat_log_bounds_kernel(
+    tc, tab_words, tab_scales, offs, offs2, offs3, wlo, whi_words, whi_scales, bhi, page0, wread, d, out
+):
+    nc = tc.nc
+    with ExitStack() as ctx:
+        keep = ctx.enter_context(tc.tile_pool(name="keep", bufs=1))
+        ring = ctx.enter_context(tc.tile_pool(name="ring", bufs=1))
+        psum = ctx.enter_context(tc.psum_pool(name="psum", bufs=8))
+
+        def held(shape, dtype, name):
+            return keep.tile(shape, dtype, name=name, align_bytes=ALIGN)
+
+        idx = keep.tile([P, S // 16], U16, name="idx")
+        idx2 = keep.tile([P, S // 16], U16, name="idx2")
+        idx3 = keep.tile([P, J // 16], U16, name="idx3")
+        tab_w = held([P, T], I32, "tab_w")
+        tab_s = held([P, T], U8, "tab_s")
+        v_w = held([P, S], U32, "v_w")
+        v_s = held([P, S], U8, "v_s")
+        whi_raw_w = held([P, 2 * H], U8, "whi_raw_w")
+        whi_raw_s = held([P, H], U8, "whi_raw_s")
+        whi_w = held([P, 2 * H], U8, "whi_w")
+        whi_s = held([P, H], U8, "whi_s")
+        wlo_w = held([P, H], U32, "wlo_w")
+        wlo_s = held([P, H], U8, "wlo_s")
+        wread_w = [held([P, H], U32, f"wread_w{a}") for a in range(2)]
+        wread_s = [held([P, H], U8, f"wread_s{a}") for a in range(2)]
+        bhi_col = held([P, 2, PACK], F32, "bhi_col")
+        d_col = held([P, 2, PACK], F32, "d_col")
+        pages = [held([P, T2], F32, f"page{s}") for s in range(SLICES)]
+
+        def load_scale_rows(engine, tile, rows):
+            engine.memset(tile[:].bitcast(I32), 0)
+            for q in range(4):
+                nc.sync.dma_start(
+                    out=tile[32 * q : 32 * q + 4, :].bitcast(I32), in_=rows[0, 4 * q : 4 * q + 4, :].bitcast(I32)
+                )
+
+        def load_page(s):
+            a, t = divmod(s, PACK)
+            rows = page0[a * PASS : (a + 1) * PASS, :].rearrange("(p t) c -> p t c", t=PACK)
+            nc.sync.dma_start(out=pages[s][:], in_=rows[:, t, :])
+
+        def load_weight(block):
+            raw = ring.tile([P, PACK, PASS], F32, name="raw", tag="raw", bufs=3, align_bytes=ALIGN)
+            nc.sync.dma_start(out=raw[:], in_=block.rearrange("(p i) c -> p i c", i=PACK))
+            return raw
+
+        def quantize_weight(raw, words, scales, groups):
+            rounded = ring.tile([P, PACK, P, PACK], BF16, name="rounded", tag="rounded", bufs=2, align_bytes=ALIGN)
+            dealt = raw[:].rearrange("p i (m t) -> p t m i", t=PACK)
+            for t0, t1 in groups:
+                nc.scalar.copy(out=rounded[:, t0:t1], in_=dealt[:, t0:t1])
+                nc.vector.quantize_mx(
+                    out=words[:, t0 * P : t1 * P].bitcast(FP8X4),
+                    scales=scales[:, t0 * P : t1 * P],
+                    in_=rounded[:, t0:t1].rearrange("p t m i -> p (t m i)"),
+                )
+
+        nc.sync.dma_start(idx2[:], offs2)
+        load_page(0)
+        nc.sync.dma_start(idx[:], offs)
+        load_scale_rows(nc.vector, tab_s, tab_scales)
+        nc.sync.dma_start(out=whi_raw_w[:].bitcast(I32), in_=whi_words[0].bitcast(I32))
+        load_scale_rows(nc.gpsimd, whi_raw_s, whi_scales)
+        nc.sync.dma_start(out=tab_w[:], in_=tab_words[0].rearrange("p n t -> p (n t)").bitcast(I32))
+        wlo_raw0 = load_weight(wlo[:, 0:PASS])
+        nc.sync.dma_start(out=bhi_col[:], in_=bhi.rearrange("(a p t) -> p a t", a=2, t=PACK))
+        for s in range(1, 4):
+            load_page(s)
+        wlo_raw1 = load_weight(wlo[:, PASS : 2 * PASS])
+        for s in range(4, SLICES):
+            load_page(s)
+        nc.sync.dma_start(idx3[:], offs3)
+        nc.sync.dma_start(out=d_col[:], in_=d.rearrange("(a p t) -> p a t", a=2, t=PACK))
+
+        def fetch_entries(s):
+            cur = ring.tile([P, S], F32, name="cur", tag="cur", bufs=3, align_bytes=ALIGN)
+            nc.vector.tensor_copy(out=cur[:], in_=pages[s][:].indirect(idx2[:]))
+            return cur
+
+        entries = {0: fetch_entries(0)}
+        nc.vector.tensor_copy(out=v_s[:], in_=tab_s[:].indirect(idx[:]))
+        nc.vector.tensor_copy(
+            out=whi_w[:].bitcast(U16).rearrange("p (a t m) -> p a t m", a=2, t=PACK),
+            in_=whi_raw_w[:].bitcast(U16).rearrange("p (a m t) -> p a t m", a=2, t=PACK),
+        )
+        nc.vector.tensor_copy(
+            out=whi_s[:].rearrange("p (a t m) -> p a t m", a=2, t=PACK),
+            in_=whi_raw_s[:].rearrange("p (a m t) -> p a t m", a=2, t=PACK),
+        )
+        nc.vector.tensor_copy(out=v_w[:], in_=tab_w[:].bitcast(U32).indirect(idx[:]))
+        quantize_weight(wlo_raw0, wlo_w[:, 0:PASS], wlo_s[:, 0:PASS], [(0, 1), (1, PACK)])
+
+        for s in range(SLICES):
+            a, t = divmod(s, PACK)
+            cols = slice(s * P, (s + 1) * P)
+            cur = entries[s]
+            lo, hi = [], []
+            for h in range(S // BANK):
+                js = slice(h * BANK, (h + 1) * BANK)
+                lo_h = psum.tile([P, BANK], F32, name="bank", tag="bank")
+                nc.tensor.matmul_mx(
+                    out=lo_h[:], lhsT=wlo_w[:, cols].bitcast(FP8X4), lhsT_scale=wlo_s[:, cols],
+                    rhs=v_w[:, js].bitcast(FP8X4), rhs_scale=v_s[:, js], start=True, stop=True,
+                )
+                lo.append(lo_h)
+            for h in range(S // BANK):
+                js = slice(h * BANK, (h + 1) * BANK)
+                hi_h = psum.tile([P, BANK], F32, name="bank", tag="bank")
+                nc.tensor.matmul_mx(
+                    out=hi_h[:], lhsT=whi_w[:, 2 * s * P : 2 * (s + 1) * P].bitcast(FP4X4), lhsT_scale=whi_s[:, cols],
+                    rhs=v_w[:, js].bitcast(FP8X4), rhs_scale=v_s[:, js], start=True, stop=True,
+                )
+                hi.append(hi_h)
+            for h in range(S // BANK):
+                js = slice(h * BANK, (h + 1) * BANK)
+                nc.vector.tensor_tensor(out=cur[:, js], in0=lo[h][:], in1=cur[:, js], op=ALU.max)
+            for h in range(S // BANK):
+                js = slice(h * BANK, (h + 1) * BANK)
+                nc.vector.scalar_tensor_tensor(
+                    out=cur[:, js], in0=hi[h][:], scalar=bhi_col[:, a, t : t + 1], in1=cur[:, js],
+                    op0=ALU.add, op1=ALU.min,
+                )
+            if s + 1 < SLICES:
+                entries[s + 1] = fetch_entries(s + 1)
+            nc.vector.tensor_copy(out=pages[s][:].indirect(idx2[:]), in_=cur[:])
+            if s == 1:
+                quantize_weight(wlo_raw1, wlo_w[:, PASS : 2 * PASS], wlo_s[:, PASS : 2 * PASS], [(0, PACK)])
+            if 2 <= s < 6:
+                ra, rh = divmod(s - 2, 2)
+                raw = load_weight(wread[ra * PASS : (ra + 1) * PASS, rh * PASS : (rh + 1) * PASS])
+                ncols = slice(rh * PASS, (rh + 1) * PASS)
+                quantize_weight(raw, wread_w[ra][:, ncols], wread_s[ra][:, ncols], [(0, PACK)])
+
+        steps = 2 * (J // CHUNK)
+        x_rounded, added, banks = {}, {}, {}
+
+        def fetch_x(k):
+            c, a = divmod(k, 2)
+            x = ring.tile([P, PACK, CHUNK], F32, name="x", tag=f"slot{k % 4}", align_bytes=ALIGN)
+            offsets = idx3[:, c * CHUNK // 16 : (c + 1) * CHUNK // 16]
+            for t in range(PACK):
+                nc.vector.tensor_copy(out=x[:, t, :], in_=pages[a * PACK + t][:].indirect(offsets))
+            xb = ring.tile([P, CHUNK, PACK], BF16, name="xb", tag=f"slot{(k + 2) % 4}", align_bytes=ALIGN)
+            nc.scalar.copy(
+                out=xb[:].rearrange("p (c i) t -> p c t i", i=4), in_=x[:].rearrange("p t (c i) -> p c t i", i=4)
+            )
+            x_rounded[k] = xb
+            dx = ring.tile([P, PACK, CHUNK], F32, name="dx", tag="dx", bufs=4, align_bytes=ALIGN)
+            for t in range(PACK):
+                nc.scalar.activation(out=dx[:, t, :], in_=x[:, t, :], func=COPY, scale=d_col[:, a, t : t + 1])
+            added[k] = dx
+
+        def multiply(k):
+            c, a = divmod(k, 2)
+            x_w = ring.tile([P, CHUNK], U32, name="x_w", tag="x_w", bufs=4, align_bytes=ALIGN)
+            x_s = ring.tile([P, CHUNK], U8, name="x_s", tag="x_s", bufs=4, align_bytes=ALIGN)
+            nc.vector.quantize_mx(
+                out=x_w[:].bitcast(FP8X4), scales=x_s[:], in_=x_rounded[k][:].rearrange("p j t -> p (j t)")
+            )
+            if a == 0:
+                banks[c] = [psum.tile([P, 2, CHUNK], F32, name="bank", tag="bank") for b in range(SLICES // 2)]
+            for s in range(SLICES):
+                b, u = divmod(s, 2)
+                cols = slice(s * P, (s + 1) * P)
+                nc.tensor.matmul_mx(
+                    out=banks[c][b][:, u, :], lhsT=wread_w[a][:, cols].bitcast(FP8X4), lhsT_scale=wread_s[a][:, cols],
+                    rhs=x_w[:].bitcast(FP8X4), rhs_scale=x_s[:], start=(a == 0 and u == 0), stop=(a == 1 and u == 1),
+                )
+
+        def finish(c):
+            for b in range(SLICES // 2):
+                a, t = divmod(2 * b, PACK)
+                res = added[2 * c + a][:, t : t + 2, :]
+                nc.vector.tensor_tensor(out=res, in0=banks[c][b][:], in1=res, op=ALU.add)
+                rows = out[a * PASS : (a + 1) * PASS, c * CHUNK : (c + 1) * CHUNK].rearrange("(p t) j -> p t j", t=PACK)
+                nc.sync.dma_start(out=rows[:, t : t + 2, :], in_=res)
+
+        for k in range(steps + 1):
+            if k < steps:
+                fetch_x(k)
+            if k >= 1:
+                multiply(k - 1)
+            if k >= 3 and k % 2 == 1:
+                finish((k - 3) // 2)
+        finish(steps // 2 - 1)

@@ -74,31 +74,32 @@ def tile_list_lifeboat_log_bounds_kernel(
             return raw
 
         def quantize_weight(raw, words, scales, groups):
-            rounded = ring.tile([P, PACK, P, PACK], BF16, name="rounded", tag="rounded", bufs=2, align_bytes=ALIGN)
+            rounded = ring.tile([P, PACK, P, PACK], BF16, name="rounded", tag="rounded", bufs=3, align_bytes=ALIGN)
             dealt = raw[:].rearrange("p i (m t) -> p t m i", t=PACK)
-            for t0, t1 in groups:
-                nc.scalar.copy(out=rounded[:, t0:t1], in_=dealt[:, t0:t1])
+            for copy, t0, t1 in groups:
+                copy(out=rounded[:, t0:t1], in_=dealt[:, t0:t1])
                 nc.vector.quantize_mx(
                     out=words[:, t0 * P : t1 * P].bitcast(FP8X4),
                     scales=scales[:, t0 * P : t1 * P],
                     in_=rounded[:, t0:t1].rearrange("p t m i -> p (t m i)"),
                 )
 
+        nc.sync.dma_start(idx[:], offs)
+        nc.sync.dma_start(out=whi_raw_w[:].bitcast(I32), in_=whi_words[0].bitcast(I32))
+        load_scale_rows(nc.vector, tab_s, tab_scales)
         nc.sync.dma_start(idx2[:], offs2)
         load_page(0)
-        nc.sync.dma_start(idx[:], offs)
-        load_scale_rows(nc.vector, tab_s, tab_scales)
-        nc.sync.dma_start(out=whi_raw_w[:].bitcast(I32), in_=whi_words[0].bitcast(I32))
-        load_scale_rows(nc.gpsimd, whi_raw_s, whi_scales)
         nc.sync.dma_start(out=tab_w[:], in_=tab_words[0].rearrange("p n t -> p (n t)").bitcast(I32))
+        load_scale_rows(nc.gpsimd, whi_raw_s, whi_scales)
         wlo_raw0 = load_weight(wlo[:, 0:PASS])
         nc.sync.dma_start(out=bhi_col[:], in_=bhi.rearrange("(a p t) -> p a t", a=2, t=PACK))
-        for s in range(1, 4):
+        load_page(1)
+        nc.sync.dma_start(idx3[:], offs3)
+        for s in range(2, 4):
             load_page(s)
         wlo_raw1 = load_weight(wlo[:, PASS : 2 * PASS])
         for s in range(4, SLICES):
             load_page(s)
-        nc.sync.dma_start(idx3[:], offs3)
         nc.sync.dma_start(out=d_col[:], in_=d.rearrange("(a p t) -> p a t", a=2, t=PACK))
 
         def fetch_entries(s):
@@ -106,18 +107,44 @@ def tile_list_lifeboat_log_bounds_kernel(
             nc.vector.tensor_copy(out=cur[:], in_=pages[s][:].indirect(idx2[:]))
             return cur
 
-        entries = {0: fetch_entries(0)}
         nc.vector.tensor_copy(out=v_s[:], in_=tab_s[:].indirect(idx[:]))
+        entries = {0: fetch_entries(0)}
         nc.vector.tensor_copy(
             out=whi_w[:].bitcast(U16).rearrange("p (a t m) -> p a t m", a=2, t=PACK),
             in_=whi_raw_w[:].bitcast(U16).rearrange("p (a m t) -> p a t m", a=2, t=PACK),
         )
+        nc.vector.tensor_copy(out=v_w[:], in_=tab_w[:].bitcast(U32).indirect(idx[:]))
         nc.vector.tensor_copy(
             out=whi_s[:].rearrange("p (a t m) -> p a t m", a=2, t=PACK),
             in_=whi_raw_s[:].rearrange("p (a m t) -> p a t m", a=2, t=PACK),
         )
-        nc.vector.tensor_copy(out=v_w[:], in_=tab_w[:].bitcast(U32).indirect(idx[:]))
-        quantize_weight(wlo_raw0, wlo_w[:, 0:PASS], wlo_s[:, 0:PASS], [(0, 1), (1, PACK)])
+        quantize_weight(wlo_raw0, wlo_w[:, 0:PASS], wlo_s[:, 0:PASS], [(nc.vector.tensor_copy, 0, 1), (nc.scalar.copy, 1, PACK)])
+
+        x = [held([P, PACK, J], F32, f"x{a}") for a in range(2)]
+        x_w = [held([P, J], U32, f"x_w{a}") for a in range(2)]
+        x_s = [held([P, J], U8, f"x_s{a}") for a in range(2)]
+        dx_early = held([P, 2, J], F32, "dx_early")
+
+        def fetch_x(s, j0, j1):
+            a, t = divmod(s, PACK)
+            nc.vector.tensor_copy(out=x[a][:, t, j0:j1], in_=pages[s][:].indirect(idx3[:, j0 // 16 : j1 // 16]))
+
+        def round_x(a, j0, j1):
+            xb = ring.tile([P, j1 - j0, PACK], BF16, name="xb", tag="rounded", bufs=3, align_bytes=ALIGN)
+            nc.scalar.copy(
+                out=xb[:].rearrange("p (c i) t -> p c t i", i=4),
+                in_=x[a][:, :, j0:j1].rearrange("p t (c i) -> p c t i", i=4),
+            )
+            return xb
+
+        def quantize_x(xb, a, j0, j1):
+            nc.vector.quantize_mx(
+                out=x_w[a][:, j0:j1].bitcast(FP8X4), scales=x_s[a][:, j0:j1], in_=xb[:].rearrange("p j t -> p (j t)")
+            )
+
+        def scale_x(s, j0, j1, dst):
+            a, t = divmod(s, PACK)
+            nc.scalar.activation(out=dst, in_=x[a][:, t, j0:j1], func=COPY, scale=d_col[:, a, t : t + 1])
 
         for s in range(SLICES):
             a, t = divmod(s, PACK)
@@ -151,41 +178,30 @@ def tile_list_lifeboat_log_bounds_kernel(
                 )
             if s + 1 < SLICES:
                 entries[s + 1] = fetch_entries(s + 1)
+            if 1 <= s < SLICES - 1:
+                fetch_x(s - 1, 0, J)
             nc.vector.tensor_copy(out=pages[s][:].indirect(idx2[:]), in_=cur[:])
+            if s == PACK:
+                for j0 in range(0, J, BANK):
+                    quantize_x(round_x(0, j0, j0 + BANK), 0, j0, j0 + BANK)
+                for t in range(PACK):
+                    scale_x(t, 0, J, x[0][:, t, :])
+            if s in (PACK + 1, PACK + 2):
+                scale_x(s - 1, 0, J, dx_early[:, s - 1 - PACK, :])
             if s == 1:
-                quantize_weight(wlo_raw1, wlo_w[:, PASS : 2 * PASS], wlo_s[:, PASS : 2 * PASS], [(0, PACK)])
+                quantize_weight(wlo_raw1, wlo_w[:, PASS : 2 * PASS], wlo_s[:, PASS : 2 * PASS], [(nc.scalar.copy, 0, PACK)])
             if 2 <= s < 6:
                 ra, rh = divmod(s - 2, 2)
                 raw = load_weight(wread[ra * PASS : (ra + 1) * PASS, rh * PASS : (rh + 1) * PASS])
                 ncols = slice(rh * PASS, (rh + 1) * PASS)
-                quantize_weight(raw, wread_w[ra][:, ncols], wread_s[ra][:, ncols], [(0, PACK)])
+                quantize_weight(raw, wread_w[ra][:, ncols], wread_s[ra][:, ncols], [(nc.scalar.copy, 0, PACK)])
 
-        steps = 2 * (J // CHUNK)
-        x_rounded, added, banks = {}, {}, {}
+        chunks = J // CHUNK
+        added = [x[0][:, 0:2, :], x[0][:, 2:4, :], dx_early[:], x[1][:, 2:4, :]]
+        rounded_x, banks = {}, {}
 
-        def fetch_x(k):
-            c, a = divmod(k, 2)
-            x = ring.tile([P, PACK, CHUNK], F32, name="x", tag=f"slot{k % 4}", align_bytes=ALIGN)
-            offsets = idx3[:, c * CHUNK // 16 : (c + 1) * CHUNK // 16]
-            for t in range(PACK):
-                nc.vector.tensor_copy(out=x[:, t, :], in_=pages[a * PACK + t][:].indirect(offsets))
-            xb = ring.tile([P, CHUNK, PACK], BF16, name="xb", tag=f"slot{(k + 2) % 4}", align_bytes=ALIGN)
-            nc.scalar.copy(
-                out=xb[:].rearrange("p (c i) t -> p c t i", i=4), in_=x[:].rearrange("p t (c i) -> p c t i", i=4)
-            )
-            x_rounded[k] = xb
-            dx = ring.tile([P, PACK, CHUNK], F32, name="dx", tag="dx", bufs=4, align_bytes=ALIGN)
-            for t in range(PACK):
-                nc.scalar.activation(out=dx[:, t, :], in_=x[:, t, :], func=COPY, scale=d_col[:, a, t : t + 1])
-            added[k] = dx
-
-        def multiply(k):
-            c, a = divmod(k, 2)
-            x_w = ring.tile([P, CHUNK], U32, name="x_w", tag="x_w", bufs=4, align_bytes=ALIGN)
-            x_s = ring.tile([P, CHUNK], U8, name="x_s", tag="x_s", bufs=4, align_bytes=ALIGN)
-            nc.vector.quantize_mx(
-                out=x_w[:].bitcast(FP8X4), scales=x_s[:], in_=x_rounded[k][:].rearrange("p j t -> p (j t)")
-            )
+        def multiply(c, a):
+            js = slice(c * CHUNK, (c + 1) * CHUNK)
             if a == 0:
                 banks[c] = [psum.tile([P, 2, CHUNK], F32, name="bank", tag="bank") for b in range(SLICES // 2)]
             for s in range(SLICES):
@@ -193,22 +209,35 @@ def tile_list_lifeboat_log_bounds_kernel(
                 cols = slice(s * P, (s + 1) * P)
                 nc.tensor.matmul_mx(
                     out=banks[c][b][:, u, :], lhsT=wread_w[a][:, cols].bitcast(FP8X4), lhsT_scale=wread_s[a][:, cols],
-                    rhs=x_w[:].bitcast(FP8X4), rhs_scale=x_s[:], start=(a == 0 and u == 0), stop=(a == 1 and u == 1),
+                    rhs=x_w[a][:, js].bitcast(FP8X4), rhs_scale=x_s[a][:, js],
+                    start=(a == 0 and u == 0), stop=(a == 1 and u == 1),
                 )
 
         def finish(c):
+            js = slice(c * CHUNK, (c + 1) * CHUNK)
             for b in range(SLICES // 2):
                 a, t = divmod(2 * b, PACK)
-                res = added[2 * c + a][:, t : t + 2, :]
+                res = added[b][:, :, js]
                 nc.vector.tensor_tensor(out=res, in0=banks[c][b][:], in1=res, op=ALU.add)
-                rows = out[a * PASS : (a + 1) * PASS, c * CHUNK : (c + 1) * CHUNK].rearrange("(p t) j -> p t j", t=PACK)
+                rows = out[a * PASS : (a + 1) * PASS, js].rearrange("(p t) j -> p t j", t=PACK)
                 nc.sync.dma_start(out=rows[:, t : t + 2, :], in_=res)
 
-        for k in range(steps + 1):
-            if k < steps:
-                fetch_x(k)
-            if k >= 1:
-                multiply(k - 1)
-            if k >= 3 and k % 2 == 1:
-                finish((k - 3) // 2)
-        finish(steps // 2 - 1)
+        for c in range(chunks):
+            j0, j1 = c * CHUNK, (c + 1) * CHUNK
+            for s in (SLICES - 2, SLICES - 1):
+                fetch_x(s, j0, j1)
+            rounded_x[c] = round_x(1, j0, j1)
+            for s in (SLICES - 2, SLICES - 1):
+                scale_x(s, j0, j1, x[1][:, s - PACK, j0:j1])
+            if c >= 1:
+                prev = c - 1
+                multiply(prev, 0)
+                quantize_x(rounded_x[prev], 1, prev * CHUNK, c * CHUNK)
+                multiply(prev, 1)
+            if c >= 2:
+                finish(c - 2)
+        multiply(chunks - 1, 0)
+        quantize_x(rounded_x[chunks - 1], 1, J - CHUNK, J)
+        multiply(chunks - 1, 1)
+        finish(chunks - 2)
+        finish(chunks - 1)

@@ -14,14 +14,12 @@ U8 = mybir.dt.uint8
 FP8X4 = mybir.dt.float8_e4m3fn_x4
 FP4X4 = mybir.dt.float4_e2m1fn_x4
 ALU = mybir.AluOpType
-COPY = mybir.ActivationFunctionType.Copy
 
 P = 128
 PACK = 4
 PASS = P * PACK
 BANK = 512
 SLICES = H // P
-CHUNK = 256
 ALIGN = 64
 
 
@@ -69,26 +67,27 @@ def tile_list_lifeboat_log_bounds_kernel(
             nc.sync.dma_start(out=pages[s][:], in_=rows[:, t, :])
 
         def load_weight(block):
-            raw = ring.tile([P, PACK, PASS], F32, name="raw", tag="raw", bufs=3, align_bytes=ALIGN)
+            raw = ring.tile([P, PACK, PASS], F32, name="raw", tag="raw", bufs=6, align_bytes=ALIGN)
             nc.sync.dma_start(out=raw[:], in_=block.rearrange("(p i) c -> p i c", i=PACK))
             return raw
 
-        def quantize_weight(raw, words, scales, groups):
-            rounded = ring.tile([P, PACK, P, PACK], BF16, name="rounded", tag="rounded", bufs=3, align_bytes=ALIGN)
-            dealt = raw[:].rearrange("p i (m t) -> p t m i", t=PACK)
-            for copy, t0, t1 in groups:
-                copy(out=rounded[:, t0:t1], in_=dealt[:, t0:t1])
+        def quantize_weight(raw, words, scales, parts=1):
+            rounded = ring.tile([P, PACK, P, PACK], BF16, name="rounded", tag="rounded", bufs=2, align_bytes=ALIGN)
+            dealt = raw[:].rearrange("p i (m t) -> p m t i", t=PACK)
+            step = PACK // parts
+            for t0 in range(0, PACK, step):
+                part = rounded[:, t0 : t0 + step]
+                cols = slice(t0 * P, (t0 + step) * P)
+                nc.scalar.copy(out=part.rearrange("p t m i -> p m t i"), in_=dealt[:, :, t0 : t0 + step])
                 nc.vector.quantize_mx(
-                    out=words[:, t0 * P : t1 * P].bitcast(FP8X4),
-                    scales=scales[:, t0 * P : t1 * P],
-                    in_=rounded[:, t0:t1].rearrange("p t m i -> p (t m i)"),
+                    out=words[:, cols].bitcast(FP8X4), scales=scales[:, cols], in_=part.rearrange("p t m i -> p (t m i)")
                 )
 
         nc.sync.dma_start(idx[:], offs)
         nc.sync.dma_start(out=whi_raw_w[:].bitcast(I32), in_=whi_words[0].bitcast(I32))
-        load_scale_rows(nc.vector, tab_s, tab_scales)
         nc.sync.dma_start(idx2[:], offs2)
         load_page(0)
+        load_scale_rows(nc.vector, tab_s, tab_scales)
         nc.sync.dma_start(out=tab_w[:], in_=tab_words[0].rearrange("p n t -> p (n t)").bitcast(I32))
         load_scale_rows(nc.gpsimd, whi_raw_s, whi_scales)
         wlo_raw0 = load_weight(wlo[:, 0:PASS])
@@ -98,53 +97,67 @@ def tile_list_lifeboat_log_bounds_kernel(
         for s in range(2, 4):
             load_page(s)
         wlo_raw1 = load_weight(wlo[:, PASS : 2 * PASS])
-        for s in range(4, SLICES):
+        for s in range(4, 6):
+            load_page(s)
+        wread_raw = [
+            load_weight(wread[a * PASS : (a + 1) * PASS, h * PASS : (h + 1) * PASS]) for a in range(2) for h in range(2)
+        ]
+        for s in range(6, SLICES):
             load_page(s)
         nc.sync.dma_start(out=d_col[:], in_=d.rearrange("(a p t) -> p a t", a=2, t=PACK))
 
         def fetch_entries(s):
-            cur = ring.tile([P, S], F32, name="cur", tag="cur", bufs=3, align_bytes=ALIGN)
+            cur = ring.tile([P, S], F32, name="cur", tag="cur", bufs=2, align_bytes=ALIGN)
             nc.vector.tensor_copy(out=cur[:], in_=pages[s][:].indirect(idx2[:]))
             return cur
 
-        nc.vector.tensor_copy(out=v_s[:], in_=tab_s[:].indirect(idx[:]))
-        entries = {0: fetch_entries(0)}
         nc.vector.tensor_copy(
             out=whi_w[:].bitcast(U16).rearrange("p (a t m) -> p a t m", a=2, t=PACK),
             in_=whi_raw_w[:].bitcast(U16).rearrange("p (a m t) -> p a t m", a=2, t=PACK),
         )
+        entries = {0: fetch_entries(0)}
+        nc.vector.tensor_copy(out=v_s[:], in_=tab_s[:].indirect(idx[:]))
         nc.vector.tensor_copy(out=v_w[:], in_=tab_w[:].bitcast(U32).indirect(idx[:]))
         nc.vector.tensor_copy(
             out=whi_s[:].rearrange("p (a t m) -> p a t m", a=2, t=PACK),
             in_=whi_raw_s[:].rearrange("p (a m t) -> p a t m", a=2, t=PACK),
         )
-        quantize_weight(wlo_raw0, wlo_w[:, 0:PASS], wlo_s[:, 0:PASS], [(nc.vector.tensor_copy, 0, 1), (nc.scalar.copy, 1, PACK)])
+        quantize_weight(wlo_raw0, wlo_w[:, 0:PASS], wlo_s[:, 0:PASS], parts=2)
 
-        x = [held([P, PACK, J], F32, f"x{a}") for a in range(2)]
-        x_w = [held([P, J], U32, f"x_w{a}") for a in range(2)]
-        x_s = [held([P, J], U8, f"x_s{a}") for a in range(2)]
-        dx_early = held([P, 2, J], F32, "dx_early")
+        x = [[held([P, PACK, BANK], F32, f"x{a}{h}") for h in range(2)] for a in range(2)]
+        x_w = [[held([P, BANK], U32, f"x_w{a}{h}") for h in range(2)] for a in range(2)]
+        x_s = [[held([P, BANK], U8, f"x_s{a}{h}") for h in range(2)] for a in range(2)]
 
-        def fetch_x(s, j0, j1):
+        def fetch_x(s, h):
             a, t = divmod(s, PACK)
-            nc.vector.tensor_copy(out=x[a][:, t, j0:j1], in_=pages[s][:].indirect(idx3[:, j0 // 16 : j1 // 16]))
+            offsets = idx3[:, h * BANK // 16 : (h + 1) * BANK // 16]
+            nc.vector.tensor_copy(out=x[a][h][:, t, :], in_=pages[s][:].indirect(offsets))
 
-        def round_x(a, j0, j1):
-            xb = ring.tile([P, j1 - j0, PACK], BF16, name="xb", tag="rounded", bufs=3, align_bytes=ALIGN)
+        def quantize_x(a, h):
+            xb = ring.tile([P, BANK, PACK], BF16, name="xb", tag="xb", bufs=2, align_bytes=ALIGN)
             nc.scalar.copy(
-                out=xb[:].rearrange("p (c i) t -> p c t i", i=4),
-                in_=x[a][:, :, j0:j1].rearrange("p t (c i) -> p c t i", i=4),
+                out=xb[:].rearrange("p (c i) t -> p c t i", i=4), in_=x[a][h][:].rearrange("p t (c i) -> p c t i", i=4)
             )
-            return xb
-
-        def quantize_x(xb, a, j0, j1):
             nc.vector.quantize_mx(
-                out=x_w[a][:, j0:j1].bitcast(FP8X4), scales=x_s[a][:, j0:j1], in_=xb[:].rearrange("p j t -> p (j t)")
+                out=x_w[a][h][:].bitcast(FP8X4), scales=x_s[a][h][:], in_=xb[:].rearrange("p j t -> p (j t)")
             )
 
-        def scale_x(s, j0, j1, dst):
+        def multiply(bank, s, a, h):
+            cols = slice(s * P, (s + 1) * P)
+            nc.tensor.matmul_mx(
+                out=bank[:], lhsT=wread_w[a][:, cols].bitcast(FP8X4), lhsT_scale=wread_s[a][:, cols],
+                rhs=x_w[a][h][:].bitcast(FP8X4), rhs_scale=x_s[a][h][:], start=(a == 0), stop=(a == 1),
+            )
+
+        def finish(bank, s, h):
             a, t = divmod(s, PACK)
-            nc.scalar.activation(out=dst, in_=x[a][:, t, j0:j1], func=COPY, scale=d_col[:, a, t : t + 1])
+            js = slice(h * BANK, (h + 1) * BANK)
+            res = x[a][h][:, t, :]
+            nc.vector.scalar_tensor_tensor(
+                out=res, in0=res, scalar=d_col[:, a, t : t + 1], in1=bank[:], op0=ALU.mult, op1=ALU.add
+            )
+            rows = out[a * PASS : (a + 1) * PASS, js].rearrange("(p t) j -> p t j", t=PACK)
+            nc.sync.dma_start(out=rows[:, t, :], in_=res)
 
         for s in range(SLICES):
             a, t = divmod(s, PACK)
@@ -178,66 +191,36 @@ def tile_list_lifeboat_log_bounds_kernel(
                 )
             if s + 1 < SLICES:
                 entries[s + 1] = fetch_entries(s + 1)
-            if 1 <= s < SLICES - 1:
-                fetch_x(s - 1, 0, J)
+            else:
+                y = [psum.tile([P, BANK], F32, name="bank", tag="bank") for n in range(SLICES)]
+                for n in range(SLICES):
+                    multiply(y[n], n, 0, 0)
+            if s >= 1:
+                fetch_x(s - 1, 0)
+                if s < SLICES - 2:
+                    fetch_x(s - 1, 1)
             nc.vector.tensor_copy(out=pages[s][:].indirect(idx2[:]), in_=cur[:])
             if s == PACK:
-                for j0 in range(0, J, BANK):
-                    quantize_x(round_x(0, j0, j0 + BANK), 0, j0, j0 + BANK)
-                for t in range(PACK):
-                    scale_x(t, 0, J, x[0][:, t, :])
-            if s in (PACK + 1, PACK + 2):
-                scale_x(s - 1, 0, J, dx_early[:, s - 1 - PACK, :])
+                for h in range(2):
+                    quantize_x(0, h)
             if s == 1:
-                quantize_weight(wlo_raw1, wlo_w[:, PASS : 2 * PASS], wlo_s[:, PASS : 2 * PASS], [(nc.scalar.copy, 0, PACK)])
+                quantize_weight(wlo_raw1, wlo_w[:, PASS : 2 * PASS], wlo_s[:, PASS : 2 * PASS])
             if 2 <= s < 6:
                 ra, rh = divmod(s - 2, 2)
-                raw = load_weight(wread[ra * PASS : (ra + 1) * PASS, rh * PASS : (rh + 1) * PASS])
                 ncols = slice(rh * PASS, (rh + 1) * PASS)
-                quantize_weight(raw, wread_w[ra][:, ncols], wread_s[ra][:, ncols], [(nc.scalar.copy, 0, PACK)])
+                quantize_weight(wread_raw[s - 2], wread_w[ra][:, ncols], wread_s[ra][:, ncols])
 
-        chunks = J // CHUNK
-        added = [x[0][:, 0:2, :], x[0][:, 2:4, :], dx_early[:], x[1][:, 2:4, :]]
-        rounded_x, banks = {}, {}
-
-        def multiply(c, a):
-            js = slice(c * CHUNK, (c + 1) * CHUNK)
-            if a == 0:
-                banks[c] = [psum.tile([P, 2, CHUNK], F32, name="bank", tag="bank") for b in range(SLICES // 2)]
-            for s in range(SLICES):
-                b, u = divmod(s, 2)
-                cols = slice(s * P, (s + 1) * P)
-                nc.tensor.matmul_mx(
-                    out=banks[c][b][:, u, :], lhsT=wread_w[a][:, cols].bitcast(FP8X4), lhsT_scale=wread_s[a][:, cols],
-                    rhs=x_w[a][:, js].bitcast(FP8X4), rhs_scale=x_s[a][:, js],
-                    start=(a == 0 and u == 0), stop=(a == 1 and u == 1),
-                )
-
-        def finish(c):
-            js = slice(c * CHUNK, (c + 1) * CHUNK)
-            for b in range(SLICES // 2):
-                a, t = divmod(2 * b, PACK)
-                res = added[b][:, :, js]
-                nc.vector.tensor_tensor(out=res, in0=banks[c][b][:], in1=res, op=ALU.add)
-                rows = out[a * PASS : (a + 1) * PASS, js].rearrange("(p t) j -> p t j", t=PACK)
-                nc.sync.dma_start(out=rows[:, t : t + 2, :], in_=res)
-
-        for c in range(chunks):
-            j0, j1 = c * CHUNK, (c + 1) * CHUNK
-            for s in (SLICES - 2, SLICES - 1):
-                fetch_x(s, j0, j1)
-            rounded_x[c] = round_x(1, j0, j1)
-            for s in (SLICES - 2, SLICES - 1):
-                scale_x(s, j0, j1, x[1][:, s - PACK, j0:j1])
-            if c >= 1:
-                prev = c - 1
-                multiply(prev, 0)
-                quantize_x(rounded_x[prev], 1, prev * CHUNK, c * CHUNK)
-                multiply(prev, 1)
-            if c >= 2:
-                finish(c - 2)
-        multiply(chunks - 1, 0)
-        quantize_x(rounded_x[chunks - 1], 1, J - CHUNK, J)
-        multiply(chunks - 1, 1)
-        finish(chunks - 2)
-        finish(chunks - 1)
+        fetch_x(SLICES - 1, 0)
+        for s in range(SLICES - 3, SLICES):
+            fetch_x(s, 1)
+        for h in range(2):
+            quantize_x(1, h)
+        for s in range(SLICES):
+            multiply(y[s], s, 1, 0)
+        for s in range(SLICES):
+            finish(y[s], s, 0)
+        for s in range(SLICES):
+            bank = psum.tile([P, BANK], F32, name="bank", tag="bank")
+            for a in range(2):
+                multiply(bank, s, a, 1)
+            finish(bank, s, 1)

from contextlib import ExitStack

import concourse.mybir as mybir

K, T, S, H, T2, J = 512, 4096, 1024, 1024, 2048, 1024
FLOPS = 2 * K * H * S * 2 + 2 * H * H * J

F32 = mybir.dt.float32
BF16 = mybir.dt.bfloat16
I32 = mybir.dt.int32
U32 = mybir.dt.uint32
U16 = mybir.dt.uint16
U8 = mybir.dt.uint8
FP8X4 = mybir.dt.float8_e4m3fn_x4
FP4X4 = mybir.dt.float4_e2m1fn_x4
ALU = mybir.AluOpType

P = 128
PACK = 4
PASS = P * PACK
BANK = 512
SLICES = H // P
ALIGN = 64


def tile_list_lifeboat_log_bounds_kernel(
    tc, tab_words, tab_scales, offs, offs2, offs3, wlo, whi_words, whi_scales, bhi, page0, wread, d, out
):
    nc = tc.nc
    with ExitStack() as ctx:
        keep = ctx.enter_context(tc.tile_pool(name="keep", bufs=1))
        ring = ctx.enter_context(tc.tile_pool(name="ring", bufs=1))
        psum = ctx.enter_context(tc.psum_pool(name="psum", bufs=8))

        def held(shape, dtype, name):
            return keep.tile(shape, dtype, name=name, align_bytes=ALIGN)

        idx = keep.tile([P, S // 16], U16, name="idx")
        idx2 = keep.tile([P, S // 16], U16, name="idx2")
        idx3 = keep.tile([P, J // 16], U16, name="idx3")
        tab_w = held([P, T], I32, "tab_w")
        tab_s = held([P, T], U8, "tab_s")
        v_w = held([P, S], U32, "v_w")
        v_s = held([P, S], U8, "v_s")
        whi_raw_w = held([P, 2 * H], U8, "whi_raw_w")
        whi_raw_s = held([P, H], U8, "whi_raw_s")
        whi_w = held([P, 2 * H], U8, "whi_w")
        whi_s = held([P, H], U8, "whi_s")
        wlo_w = held([P, H], U32, "wlo_w")
        wlo_s = held([P, H], U8, "wlo_s")
        wread_w = [held([P, H], U32, f"wread_w{a}") for a in range(2)]
        wread_s = [held([P, H], U8, f"wread_s{a}") for a in range(2)]
        bhi_col = held([P, 2, PACK], F32, "bhi_col")
        d_col = held([P, 2, PACK], F32, "d_col")
        pages = [held([P, T2], F32, f"page{s}") for s in range(SLICES)]

        def load_scale_rows(engine, tile, rows):
            engine.memset(tile[:].bitcast(I32), 0)
            for q in range(4):
                nc.sync.dma_start(
                    out=tile[32 * q : 32 * q + 4, :].bitcast(I32), in_=rows[0, 4 * q : 4 * q + 4, :].bitcast(I32)
                )

        def load_page(s):
            a, t = divmod(s, PACK)
            rows = page0[a * PASS : (a + 1) * PASS, :].rearrange("(p t) c -> p t c", t=PACK)
            nc.sync.dma_start(out=pages[s][:], in_=rows[:, t, :])

        def load_weight(block):
            raw = ring.tile([P, PACK, PASS], F32, name="raw", tag="raw", bufs=6, align_bytes=ALIGN)
            nc.sync.dma_start(out=raw[:], in_=block.rearrange("(p i) c -> p i c", i=PACK))
            return raw

        def quantize_weight(raw, words, scales, parts=1):
            rounded = ring.tile([P, PACK, P, PACK], BF16, name="rounded", tag="rounded", bufs=2, align_bytes=ALIGN)
            dealt = raw[:].rearrange("p i (m t) -> p m t i", t=PACK)
            step = PACK // parts
            for t0 in range(0, PACK, step):
                part = rounded[:, t0 : t0 + step]
                cols = slice(t0 * P, (t0 + step) * P)
                nc.scalar.copy(out=part.rearrange("p t m i -> p m t i"), in_=dealt[:, :, t0 : t0 + step])
                nc.vector.quantize_mx(
                    out=words[:, cols].bitcast(FP8X4), scales=scales[:, cols], in_=part.rearrange("p t m i -> p (t m i)")
                )

        nc.sync.dma_start(idx[:], offs)
        nc.sync.dma_start(out=whi_raw_w[:].bitcast(I32), in_=whi_words[0].bitcast(I32))
        nc.sync.dma_start(idx2[:], offs2)
        load_page(0)
        load_scale_rows(nc.vector, tab_s, tab_scales)
        nc.sync.dma_start(out=tab_w[:], in_=tab_words[0].rearrange("p n t -> p (n t)").bitcast(I32))
        load_scale_rows(nc.gpsimd, whi_raw_s, whi_scales)
        wlo_raw0 = load_weight(wlo[:, 0:PASS])
        nc.sync.dma_start(out=bhi_col[:], in_=bhi.rearrange("(a p t) -> p a t", a=2, t=PACK))
        load_page(1)
        nc.sync.dma_start(idx3[:], offs3)
        for s in range(2, 4):
            load_page(s)
        wlo_raw1 = load_weight(wlo[:, PASS : 2 * PASS])
        for s in range(4, 6):
            load_page(s)
        wread_raw = [
            load_weight(wread[a * PASS : (a + 1) * PASS, h * PASS : (h + 1) * PASS]) for a in range(2) for h in range(2)
        ]
        for s in range(6, SLICES):
            load_page(s)
        nc.sync.dma_start(out=d_col[:], in_=d.rearrange("(a p t) -> p a t", a=2, t=PACK))

        def fetch_entries(s):
            cur = ring.tile([P, S], F32, name="cur", tag="cur", bufs=2, align_bytes=ALIGN)
            nc.vector.tensor_copy(out=cur[:], in_=pages[s][:].indirect(idx2[:]))
            return cur

        nc.vector.tensor_copy(
            out=whi_w[:].bitcast(U16).rearrange("p (a t m) -> p a t m", a=2, t=PACK),
            in_=whi_raw_w[:].bitcast(U16).rearrange("p (a m t) -> p a t m", a=2, t=PACK),
        )
        entries = {0: fetch_entries(0)}
        nc.vector.tensor_copy(out=v_s[:], in_=tab_s[:].indirect(idx[:]))
        nc.vector.tensor_copy(out=v_w[:], in_=tab_w[:].bitcast(U32).indirect(idx[:]))
        nc.vector.tensor_copy(
            out=whi_s[:].rearrange("p (a t m) -> p a t m", a=2, t=PACK),
            in_=whi_raw_s[:].rearrange("p (a m t) -> p a t m", a=2, t=PACK),
        )
        quantize_weight(wlo_raw0, wlo_w[:, 0:PASS], wlo_s[:, 0:PASS], parts=2)

        x = [[held([P, PACK, BANK], F32, f"x{a}{h}") for h in range(2)] for a in range(2)]
        x_w = [[held([P, BANK], U32, f"x_w{a}{h}") for h in range(2)] for a in range(2)]
        x_s = [[held([P, BANK], U8, f"x_s{a}{h}") for h in range(2)] for a in range(2)]

        def fetch_x(s, h):
            a, t = divmod(s, PACK)
            offsets = idx3[:, h * BANK // 16 : (h + 1) * BANK // 16]
            nc.vector.tensor_copy(out=x[a][h][:, t, :], in_=pages[s][:].indirect(offsets))

        def quantize_x(a, h):
            xb = ring.tile([P, BANK, PACK], BF16, name="xb", tag="xb", bufs=2, align_bytes=ALIGN)
            nc.scalar.copy(
                out=xb[:].rearrange("p (c i) t -> p c t i", i=4), in_=x[a][h][:].rearrange("p t (c i) -> p c t i", i=4)
            )
            nc.vector.quantize_mx(
                out=x_w[a][h][:].bitcast(FP8X4), scales=x_s[a][h][:], in_=xb[:].rearrange("p j t -> p (j t)")
            )

        def multiply(bank, s, a, h):
            cols = slice(s * P, (s + 1) * P)
            nc.tensor.matmul_mx(
                out=bank[:], lhsT=wread_w[a][:, cols].bitcast(FP8X4), lhsT_scale=wread_s[a][:, cols],
                rhs=x_w[a][h][:].bitcast(FP8X4), rhs_scale=x_s[a][h][:], start=(a == 0), stop=(a == 1),
            )

        def finish(bank, s, h):
            a, t = divmod(s, PACK)
            js = slice(h * BANK, (h + 1) * BANK)
            res = x[a][h][:, t, :]
            nc.vector.scalar_tensor_tensor(
                out=res, in0=res, scalar=d_col[:, a, t : t + 1], in1=bank[:], op0=ALU.mult, op1=ALU.add
            )
            rows = out[a * PASS : (a + 1) * PASS, js].rearrange("(p t) j -> p t j", t=PACK)
            nc.sync.dma_start(out=rows[:, t, :], in_=res)

        for s in range(SLICES):
            a, t = divmod(s, PACK)
            cols = slice(s * P, (s + 1) * P)
            cur = entries[s]
            lo, hi = [], []
            for h in range(S // BANK):
                js = slice(h * BANK, (h + 1) * BANK)
                lo_h = psum.tile([P, BANK], F32, name="bank", tag="bank")
                nc.tensor.matmul_mx(
                    out=lo_h[:], lhsT=wlo_w[:, cols].bitcast(FP8X4), lhsT_scale=wlo_s[:, cols],
                    rhs=v_w[:, js].bitcast(FP8X4), rhs_scale=v_s[:, js], start=True, stop=True,
                )
                lo.append(lo_h)
            for h in range(S // BANK):
                js = slice(h * BANK, (h + 1) * BANK)
                hi_h = psum.tile([P, BANK], F32, name="bank", tag="bank")
                nc.tensor.matmul_mx(
                    out=hi_h[:], lhsT=whi_w[:, 2 * s * P : 2 * (s + 1) * P].bitcast(FP4X4), lhsT_scale=whi_s[:, cols],
                    rhs=v_w[:, js].bitcast(FP8X4), rhs_scale=v_s[:, js], start=True, stop=True,
                )
                hi.append(hi_h)
            for h in range(S // BANK):
                js = slice(h * BANK, (h + 1) * BANK)
                nc.vector.tensor_tensor(out=cur[:, js], in0=lo[h][:], in1=cur[:, js], op=ALU.max)
            for h in range(S // BANK):
                js = slice(h * BANK, (h + 1) * BANK)
                nc.vector.scalar_tensor_tensor(
                    out=cur[:, js], in0=hi[h][:], scalar=bhi_col[:, a, t : t + 1], in1=cur[:, js],
                    op0=ALU.add, op1=ALU.min,
                )
            if s + 1 < SLICES:
                entries[s + 1] = fetch_entries(s + 1)
            else:
                y = [psum.tile([P, BANK], F32, name="bank", tag="bank") for n in range(SLICES)]
                for n in range(SLICES):
                    multiply(y[n], n, 0, 0)
            if s >= 1:
                fetch_x(s - 1, 0)
                if s < SLICES - 2:
                    fetch_x(s - 1, 1)
            nc.vector.tensor_copy(out=pages[s][:].indirect(idx2[:]), in_=cur[:])
            if s == PACK:
                for h in range(2):
                    quantize_x(0, h)
            if s == 1:
                quantize_weight(wlo_raw1, wlo_w[:, PASS : 2 * PASS], wlo_s[:, PASS : 2 * PASS])
            if 2 <= s < 6:
                ra, rh = divmod(s - 2, 2)
                ncols = slice(rh * PASS, (rh + 1) * PASS)
                quantize_weight(wread_raw[s - 2], wread_w[ra][:, ncols], wread_s[ra][:, ncols])

        fetch_x(SLICES - 1, 0)
        for s in range(SLICES - 3, SLICES):
            fetch_x(s, 1)
        for h in range(2):
            quantize_x(1, h)
        for s in range(SLICES):
            multiply(y[s], s, 1, 0)
        for s in range(SLICES):
            finish(y[s], s, 0)
        for s in range(SLICES):
            bank = psum.tile([P, BANK], F32, name="bank", tag="bank")
            for a in range(2):
                multiply(bank, s, a, 1)
            finish(bank, s, 1)
